import numpy as np, ml_dtypes
CORES = [127,119,111,103,95,87,79,71,63,55,47,39,31,23,15,7]
N = 16
def setup_inputs(rng):
    return {"x": rng.standard_normal((N, 128, 256), dtype=np.float32).astype(ml_dtypes.bfloat16)}
def reference(x):
    s = np.maximum.accumulate(x, axis=0)
    y = np.full(x.shape, np.nan, x.dtype)
    y[1:] = s[:-1]
    return {"y": y}

@@ -1,0 +1,81 @@
+from concourse.bass import DstId, RemoteDMATransfer
+
+L = 8
+W = 256 // L
+S = 1
+HELP = [6, 5, 4, 3, 2, 1, 0]
+E1 = max(1, 8 // L)
+
+SCRATCH = {
+    "xs": ("dram", [L, 128, W], "bfloat16"),
+    "land": ("dram", [15, 128, W], "bfloat16"),
+    "res": ("dram", [L, 128, W], "bfloat16"),
+}
+SEMAPHORES = ["loaded", "sent", "arrived", "got", "stored"]
+
+
+def fold_plan(cores):
+    plan = {}
+    for p in range(L):
+        for par in (0, 1):
+            tg = [r for r in range(1, 16) if (cores[r] // 8) % 2 == par]
+            chunk = -(-len(tg) // S)
+            for s in range(S):
+                sub = tg[s * chunk:(s + 1) * chunk]
+                e = 1
+                while e * 2 * len(sub) <= 8:
+                    e *= 2
+                c = (2 * (p % 8) + par) * 8 + HELP[(p // 8) * S + s]
+                plan[c] = (p, [(j, e) for j in sub], max(sub))
+    return plan
+
+
+def dst_id(topo, c):
+    rid, pid, _se = topo.addr(c)
+    return DstId(rid=rid, pnc=pid)
+
+
+def rank_program(g, core, T, topo):
+    plan = fold_plan(T.cores)
+    rank = T.rank_of(core)
+
+    if rank is None:
+        if core not in plan:
+            return
+        p, targets, nsrc = plan[core]
+        g.wait_ge(T.sem.arrived, nsrc * E1)
+        trs = []
+        eng = 0
+        for j, e in targets:
+            mask = ((1 << e) - 1) << eng
+            eng += e
+            trs.append(RemoteDMATransfer(
+                dst_ids=[dst_id(topo, T.cores[j])], dma_engine_mask=mask, remote_sem=T.sem.got,
+                srcs=[T.land[i] for i in range(j)], dsts=[T.res[p]], alu_op=2 if j > 1 else 0))
+        g.remote_dma_fused(trs, local_sem=T.sem.sent)
+        g.wait_ge(T.sem.sent, eng)
+        return
+
+    if rank <= 14:
+        g.sync.dma_start(T.xs[:], T.x[:]).then_inc(T.sem.loaded, 16)
+        g.wait_ge(T.sem.loaded, 16)
+        sent = 0
+        for p0 in range(0, L, 8):
+            trs = []
+            for p in range(p0, min(L, p0 + 8)):
+                to = [c for c in sorted(plan) if plan[c][0] == p and rank < plan[c][2]]
+                if not to:
+                    continue
+                mask = ((1 << E1) - 1) << ((p - p0) * E1)
+                trs.append(RemoteDMATransfer(
+                    dst_ids=[dst_id(topo, c) for c in to], dma_engine_mask=mask, remote_sem=T.sem.arrived,
+                    srcs=[T.xs[p]], dsts=[T.land[rank] for c in to], alu_op=0))
+                sent += E1
+            g.remote_dma_fused(trs, local_sem=T.sem.sent)
+    if rank >= 1:
+        e = [ee for c in plan for (j, ee) in plan[c][1] if j == rank][0]
+        g.sync.wait_ge(T.sem.got, L * e)
+        g.sync.dma_start(T.y[:], T.res[:]).then_inc(T.sem.stored, 16)
+        g.sync.wait_ge(T.sem.stored, 16)
+    if rank <= 14:
+        g.wait_ge(T.sem.sent, sent)

@@ -1,10 +1,9 @@
 from concourse.bass import DstId, RemoteDMATransfer
 
-L = 8
+L = 16
+D = 2
 W = 256 // L
-S = 1
-HELP = [6, 5, 4, 3, 2, 1, 0]
-E1 = max(1, 8 // L)
+HELP = [6, 5, 4, 3, 2, 1, 0] if D == 2 else [6, 3, 2]
 
 SCRATCH = {
     "xs": ("dram", [L, 128, W], "bfloat16"),
@@ -17,16 +16,17 @@ SEMAPHORES = ["loaded", "sent", "arrived", "got", "stored"]
 def fold_plan(cores):
     plan = {}
     for p in range(L):
+        if D == 1:
+            c = (p % 16) * 8 + HELP[p // 16]
+            calls = [[(15 - k, k, 1) for k in range(8)], [(k, k, 1) for k in range(1, 8)]]
+            plan[c] = (p, calls, 15)
+            continue
         for par in (0, 1):
-            tg = [r for r in range(1, 16) if (cores[r] // 8) % 2 == par]
-            chunk = -(-len(tg) // S)
-            for s in range(S):
-                sub = tg[s * chunk:(s + 1) * chunk]
-                e = 1
-                while e * 2 * len(sub) <= 8:
-                    e *= 2
-                c = (2 * (p % 8) + par) * 8 + HELP[(p // 8) * S + s]
-                plan[c] = (p, [(j, e) for j in sub], max(sub))
+            tg = sorted([r for r in range(1, 16) if (cores[r] // 8) % 2 == par], reverse=True)
+            hi, lo = tg[:4], sorted(tg[4:])
+            calls = [[(j, 2 * k, 2) for k, j in enumerate(hi)], [(j, 2 * k, 2) for k, j in enumerate(lo)]]
+            c = (2 * (p % 8) + par) * 8 + HELP[p // 8]
+            plan[c] = (p, calls, max(tg))
     return plan
 
 
@@ -42,18 +42,18 @@ def rank_program(g, core, T, topo):
     if rank is None:
         if core not in plan:
             return
-        p, targets, nsrc = plan[core]
-        g.wait_ge(T.sem.arrived, nsrc * E1)
-        trs = []
-        eng = 0
-        for j, e in targets:
-            mask = ((1 << e) - 1) << eng
-            eng += e
-            trs.append(RemoteDMATransfer(
-                dst_ids=[dst_id(topo, T.cores[j])], dma_engine_mask=mask, remote_sem=T.sem.got,
-                srcs=[T.land[i] for i in range(j)], dsts=[T.res[p]], alu_op=2 if j > 1 else 0))
-        g.remote_dma_fused(trs, local_sem=T.sem.sent)
-        g.wait_ge(T.sem.sent, eng)
+        p, calls, nsrc = plan[core]
+        g.wait_ge(T.sem.arrived, nsrc)
+        sent = 0
+        for call in calls:
+            trs = []
+            for j, e0, e in call:
+                sent += e
+                trs.append(RemoteDMATransfer(
+                    dst_ids=[dst_id(topo, T.cores[j])], dma_engine_mask=((1 << e) - 1) << e0, remote_sem=T.sem.got,
+                    srcs=[T.land[i] for i in range(j)], dsts=[T.res[p]], alu_op=2 if j > 1 else 0))
+            g.remote_dma_fused(trs, local_sem=T.sem.sent)
+        g.wait_ge(T.sem.sent, sent)
         return
 
     if rank <= 14:
@@ -62,19 +62,18 @@ def rank_program(g, core, T, topo):
         sent = 0
         for p0 in range(0, L, 8):
             trs = []
-            for p in range(p0, min(L, p0 + 8)):
+            for p in range(p0, p0 + 8):
                 to = [c for c in sorted(plan) if plan[c][0] == p and rank < plan[c][2]]
                 if not to:
                     continue
-                mask = ((1 << E1) - 1) << ((p - p0) * E1)
                 trs.append(RemoteDMATransfer(
-                    dst_ids=[dst_id(topo, c) for c in to], dma_engine_mask=mask, remote_sem=T.sem.arrived,
+                    dst_ids=[dst_id(topo, c) for c in to], dma_engine_mask=1 << (p - p0), remote_sem=T.sem.arrived,
                     srcs=[T.xs[p]], dsts=[T.land[rank] for c in to], alu_op=0))
-                sent += E1
+                sent += 1
             g.remote_dma_fused(trs, local_sem=T.sem.sent)
     if rank >= 1:
-        e = [ee for c in plan for (j, ee) in plan[c][1] if j == rank][0]
-        g.sync.wait_ge(T.sem.got, L * e)
+        got = sum(e for c in plan for call in plan[c][1] for (j, e0, e) in call if j == rank)
+        g.sync.wait_ge(T.sem.got, got)
         g.sync.dma_start(T.y[:], T.res[:]).then_inc(T.sem.stored, 16)
         g.sync.wait_ge(T.sem.stored, 16)
     if rank <= 14:

@@ -1,32 +1,31 @@
 from concourse.bass import DstId, RemoteDMATransfer
 
-L = 16
-D = 2
-W = 256 // L
-HELP = [6, 5, 4, 3, 2, 1, 0] if D == 2 else [6, 3, 2]
+WAVES = [(18, 2, [6]), (14, 4, [5, 4])]
 
-SCRATCH = {
-    "xs": ("dram", [L, 128, W], "bfloat16"),
-    "land": ("dram", [15, 128, W], "bfloat16"),
-    "res": ("dram", [L, 128, W], "bfloat16"),
-}
-SEMAPHORES = ["loaded", "sent", "arrived", "got", "stored"]
+SCRATCH = {}
+SEMAPHORES = ["sent", "arrived"]
+for _k, (_n, _d, _h) in enumerate(WAVES):
+    SCRATCH["xs%d" % _k] = ("dram", [8, 128, _n], "bfloat16")
+    SCRATCH["land%d" % _k] = ("dram", [15, 128, _n], "bfloat16")
+    SCRATCH["res%d" % _k] = ("dram", [8, 128, _n], "bfloat16")
+    SEMAPHORES += ["loaded%d" % _k, "got%d" % _k, "stored%d" % _k]
 
 
 def fold_plan(cores):
     plan = {}
-    for p in range(L):
-        if D == 1:
-            c = (p % 16) * 8 + HELP[p // 16]
-            calls = [[(15 - k, k, 1) for k in range(8)], [(k, k, 1) for k in range(1, 8)]]
-            plan[c] = (p, calls, 15)
-            continue
-        for par in (0, 1):
-            tg = sorted([r for r in range(1, 16) if (cores[r] // 8) % 2 == par], reverse=True)
-            hi, lo = tg[:4], sorted(tg[4:])
-            calls = [[(j, 2 * k, 2) for k, j in enumerate(hi)], [(j, 2 * k, 2) for k, j in enumerate(lo)]]
-            c = (2 * (p % 8) + par) * 8 + HELP[p // 8]
-            plan[c] = (p, calls, max(tg))
+    for k, (n, d, help_cores) in enumerate(WAVES):
+        for p in range(8):
+            for par in (0, 1):
+                tg = sorted([r for r in range(1, 16) if (cores[r] // 8) % 2 == par], reverse=True)
+                total = tg[0] + (1 if tg[0] == 15 else 0)
+                m = d // 2
+                nh = 4 // m
+                e = 8 // nh
+                for s in range(m):
+                    hi = tg[s * nh:(s + 1) * nh]
+                    first = [(h, i * e, e) for i, h in enumerate(hi)]
+                    second = [(total - h, i * e, e) for i, h in enumerate(hi) if total - h >= 1]
+                    plan[(2 * p + par) * 8 + help_cores[s]] = (k, p, [first, second], max(hi))
     return plan
 
 
@@ -42,7 +41,8 @@ def rank_program(g, core, T, topo):
     if rank is None:
         if core not in plan:
             return
-        p, calls, nsrc = plan[core]
+        k, p, calls, nsrc = plan[core]
+        land, res = T["land%d" % k], T["res%d" % k]
         g.wait_ge(T.sem.arrived, nsrc)
         sent = 0
         for call in calls:
@@ -50,31 +50,37 @@ def rank_program(g, core, T, topo):
             for j, e0, e in call:
                 sent += e
                 trs.append(RemoteDMATransfer(
-                    dst_ids=[dst_id(topo, T.cores[j])], dma_engine_mask=((1 << e) - 1) << e0, remote_sem=T.sem.got,
-                    srcs=[T.land[i] for i in range(j)], dsts=[T.res[p]], alu_op=2 if j > 1 else 0))
+                    dst_ids=[dst_id(topo, T.cores[j])], dma_engine_mask=((1 << e) - 1) << e0,
+                    remote_sem=T.sem["got%d" % k],
+                    srcs=[land[i] for i in range(j)], dsts=[res[p]], alu_op=2 if j > 1 else 0))
             g.remote_dma_fused(trs, local_sem=T.sem.sent)
         g.wait_ge(T.sem.sent, sent)
         return
 
+    queues = [g.sync, g.scalar]
+    rows = [0]
+    for n, d, h in WAVES:
+        rows.append(rows[-1] + 4 * n)
     if rank <= 14:
-        g.sync.dma_start(T.xs[:], T.x[:]).then_inc(T.sem.loaded, 16)
-        g.wait_ge(T.sem.loaded, 16)
+        for k in range(len(WAVES)):
+            queues[k].dma_start(T["xs%d" % k][:], T.x[rows[k]:rows[k + 1], :]).then_inc(T.sem["loaded%d" % k], 16)
         sent = 0
-        for p0 in range(0, L, 8):
+        for k in range(len(WAVES)):
+            g.wait_ge(T.sem["loaded%d" % k], 16)
             trs = []
-            for p in range(p0, p0 + 8):
-                to = [c for c in sorted(plan) if plan[c][0] == p and rank < plan[c][2]]
-                if not to:
-                    continue
+            for p in range(8):
+                to = [c for c in sorted(plan) if plan[c][0] == k and plan[c][1] == p and rank < plan[c][3]]
                 trs.append(RemoteDMATransfer(
-                    dst_ids=[dst_id(topo, c) for c in to], dma_engine_mask=1 << (p - p0), remote_sem=T.sem.arrived,
-                    srcs=[T.xs[p]], dsts=[T.land[rank] for c in to], alu_op=0))
+                    dst_ids=[dst_id(topo, c) for c in to], dma_engine_mask=1 << p, remote_sem=T.sem.arrived,
+                    srcs=[T["xs%d" % k][p]], dsts=[T["land%d" % k][rank] for c in to], alu_op=0))
                 sent += 1
             g.remote_dma_fused(trs, local_sem=T.sem.sent)
     if rank >= 1:
-        got = sum(e for c in plan for call in plan[c][1] for (j, e0, e) in call if j == rank)
-        g.sync.wait_ge(T.sem.got, got)
-        g.sync.dma_start(T.y[:], T.res[:]).then_inc(T.sem.stored, 16)
-        g.sync.wait_ge(T.sem.stored, 16)
+        for k in range(len(WAVES)):
+            got = sum(e for c in plan if plan[c][0] == k for call in plan[c][2] for (j, e0, e) in call if j == rank)
+            q = queues[k]
+            q.wait_ge(T.sem["got%d" % k], got)
+            q.dma_start(T.y[rows[k]:rows[k + 1], :], T["res%d" % k][:]).then_inc(T.sem["stored%d" % k], 16)
+            q.wait_ge(T.sem["stored%d" % k], 16)
     if rank <= 14:
         g.wait_ge(T.sem.sent, sent)

@@ -1,6 +1,6 @@
 from concourse.bass import DstId, RemoteDMATransfer
 
-WAVES = [(18, 2, [6]), (14, 4, [5, 4])]
+WAVES = [(16, 2, [6]), (16, 4, [5, 4])]
 
 SCRATCH = {}
 SEMAPHORES = ["sent", "arrived"]

from concourse.bass import DstId, RemoteDMATransfer

WAVES = [(16, 2, [6]), (16, 4, [5, 4])]

SCRATCH = {}
SEMAPHORES = ["sent", "arrived"]
for _k, (_n, _d, _h) in enumerate(WAVES):
    SCRATCH["xs%d" % _k] = ("dram", [8, 128, _n], "bfloat16")
    SCRATCH["land%d" % _k] = ("dram", [15, 128, _n], "bfloat16")
    SCRATCH["res%d" % _k] = ("dram", [8, 128, _n], "bfloat16")
    SEMAPHORES += ["loaded%d" % _k, "got%d" % _k, "stored%d" % _k]


def fold_plan(cores):
    plan = {}
    for k, (n, d, help_cores) in enumerate(WAVES):
        for p in range(8):
            for par in (0, 1):
                tg = sorted([r for r in range(1, 16) if (cores[r] // 8) % 2 == par], reverse=True)
                total = tg[0] + (1 if tg[0] == 15 else 0)
                m = d // 2
                nh = 4 // m
                e = 8 // nh
                for s in range(m):
                    hi = tg[s * nh:(s + 1) * nh]
                    first = [(h, i * e, e) for i, h in enumerate(hi)]
                    second = [(total - h, i * e, e) for i, h in enumerate(hi) if total - h >= 1]
                    plan[(2 * p + par) * 8 + help_cores[s]] = (k, p, [first, second], max(hi))
    return plan


def dst_id(topo, c):
    rid, pid, _se = topo.addr(c)
    return DstId(rid=rid, pnc=pid)


def rank_program(g, core, T, topo):
    plan = fold_plan(T.cores)
    rank = T.rank_of(core)

    if rank is None:
        if core not in plan:
            return
        k, p, calls, nsrc = plan[core]
        land, res = T["land%d" % k], T["res%d" % k]
        g.wait_ge(T.sem.arrived, nsrc)
        sent = 0
        for call in calls:
            trs = []
            for j, e0, e in call:
                sent += e
                trs.append(RemoteDMATransfer(
                    dst_ids=[dst_id(topo, T.cores[j])], dma_engine_mask=((1 << e) - 1) << e0,
                    remote_sem=T.sem["got%d" % k],
                    srcs=[land[i] for i in range(j)], dsts=[res[p]], alu_op=2 if j > 1 else 0))
            g.remote_dma_fused(trs, local_sem=T.sem.sent)
        g.wait_ge(T.sem.sent, sent)
        return

    queues = [g.sync, g.scalar]
    rows = [0]
    for n, d, h in WAVES:
        rows.append(rows[-1] + 4 * n)
    if rank <= 14:
        for k in range(len(WAVES)):
            queues[k].dma_start(T["xs%d" % k][:], T.x[rows[k]:rows[k + 1], :]).then_inc(T.sem["loaded%d" % k], 16)
        sent = 0
        for k in range(len(WAVES)):
            g.wait_ge(T.sem["loaded%d" % k], 16)
            trs = []
            for p in range(8):
                to = [c for c in sorted(plan) if plan[c][0] == k and plan[c][1] == p and rank < plan[c][3]]
                trs.append(RemoteDMATransfer(
                    dst_ids=[dst_id(topo, c) for c in to], dma_engine_mask=1 << p, remote_sem=T.sem.arrived,
                    srcs=[T["xs%d" % k][p]], dsts=[T["land%d" % k][rank] for c in to], alu_op=0))
                sent += 1
            g.remote_dma_fused(trs, local_sem=T.sem.sent)
    if rank >= 1:
        for k in range(len(WAVES)):
            got = sum(e for c in plan if plan[c][0] == k for call in plan[c][2] for (j, e0, e) in call if j == rank)
            q = queues[k]
            q.wait_ge(T.sem["got%d" % k], got)
            q.dma_start(T.y[rows[k]:rows[k + 1], :], T["res%d" % k][:]).then_inc(T.sem["stored%d" % k], 16)
            q.wait_ge(T.sem["stored%d" % k], 16)
    if rank <= 14:
        g.wait_ge(T.sem.sent, sent)
